import numpy as np
import ml_dtypes


def mxq(x, axis, fmt="e4m3"):
    dtype, down = {"e4m3": (ml_dtypes.float8_e4m3fn, 7), "e5m2": (ml_dtypes.float8_e5m2, 14)}[fmt]
    v = np.moveaxis(np.asarray(x, np.float32).astype(ml_dtypes.bfloat16).astype(np.float64), axis, -1)
    blocks = v.reshape(v.shape[:-1] + (-1, 32))
    amax = np.abs(blocks).max(-1, keepdims=True)
    byte = np.maximum(np.where(amax > 0, np.frexp(amax)[1] - 1 + 127, 0) - down, 1)
    scale = np.exp2(byte - 127.0)
    codes = (blocks / scale).astype(np.float32).astype(dtype).astype(np.float64)
    return np.moveaxis((codes * scale).reshape(v.shape), -1, axis)


WIDE = False


def mx_kscale(k):
    if not WIDE:
        return np.ones(k)
    levels = np.array([10, -10, 5, -5, 0])
    if k % 512:
        return np.exp2(np.random.permutation(np.resize(levels, k // 32))).repeat(32)
    a = np.empty((k // 512, 16))
    for p in range(k // 512):
        a[p, :8] = np.random.permutation(np.resize(levels, 8))
        for g in range(8):
            far = levels[np.abs(levels - a[p, g]) >= 10]
            a[p, g + 8] = far[np.random.randint(len(far))]
    return np.exp2(a.ravel()).repeat(32)


def f64(x):
    return np.asarray(x).astype(np.float64)


def striped(idx):
    return np.tile(idx.reshape(-1, 16).T, (8, 1)).astype(np.uint16)


def unstriped(offs):
    return offs[:16].T.reshape(-1).astype(np.int64)


def pack_weight(w):
    k, n = w.shape
    w = f64(np.asarray(w, np.float32).astype(ml_dtypes.bfloat16)).reshape(k // 32, 32, n)
    amax = np.abs(w).max(1)
    byte = np.clip(np.where(amax > 0, np.frexp(amax)[1] - 1 + 127 - 7, 1), 1, 254)
    scaled = (w * np.exp2(127.0 - byte)[:, None, :]).reshape(k, n).astype(np.float32)
    words = np.ascontiguousarray(scaled.reshape(k // 512, 128, 4, n).transpose(0, 1, 3, 2)).astype(ml_dtypes.float8_e4m3fn).view(np.uint8)
    return words, np.ascontiguousarray(byte.astype(np.uint8).reshape(k // 512, 16, n))


def unpack_weight(words, scales):
    g, p, n, _ = words.shape
    vals = np.ascontiguousarray(words).view(ml_dtypes.float8_e4m3fn).astype(np.float64) * np.repeat(np.exp2(scales.astype(np.float64) - 127.0), 8, axis=1)[..., None]
    return vals.transpose(0, 1, 3, 2).reshape(g * 512, n)


K, T, S, J = 512, 2048, 512, 512


def setup_inputs():
    n = np.random.standard_normal
    s = mx_kscale(K)[:, None]
    packed_xT = pack_weight(n((K, T)) * s)
    packed_eT = pack_weight(n((K, T)) * s)
    packed_fT = pack_weight(n((K, T)) * s)
    return {
        "x_words": packed_xT[0],
        "x_scales": packed_xT[1],
        "e_words": packed_eT[0],
        "e_scales": packed_eT[1],
        "f_words": packed_fT[0],
        "f_scales": packed_fT[1],
        "hT": (n((K, J)) / np.sqrt(3 * K) / s).astype(np.float32),
        "gT": (n((K, J)) / np.sqrt(3 * K) / s).astype(np.float32),
        "rT": (n((K, J)) / np.sqrt(3 * K) / s).astype(np.float32),
        "offs": striped(np.random.permutation(T)[:S]),
        "code2": striped(np.random.permutation(T)[:S]),
        "code3": striped(np.random.permutation(T)[:S]),
    }


def reference(x_words, x_scales, e_words, e_scales, f_words, f_scales, hT, gT, rT, offs, code2, code3):
    hTq = mxq(f64(hT), 0, "e4m3")
    xq = unpack_weight(x_words, x_scales)[:, unstriped(offs)]
    gTq = mxq(f64(gT), 0, "e4m3")
    e_code2 = unpack_weight(e_words, e_scales)[:, unstriped(code2)]
    rTq = mxq(f64(rT), 0, "e4m3")
    f_code3 = unpack_weight(f_words, f_scales)[:, unstriped(code3)]
    y = hTq.T @ xq + gTq.T @ e_code2 + rTq.T @ f_code3
    e = np.exp(y - y.max(axis=1, keepdims=True))
    return e / e.sum(axis=1, keepdims=True)

@@ -1,0 +1,229 @@
+from contextlib import ExitStack
+
+import concourse.mybir as mybir
+
+K, T, S, J = 512, 2048, 512, 512
+FLOPS = 2 * 3 * K * S * J
+
+F32 = mybir.dt.float32
+BF16 = mybir.dt.bfloat16
+I32 = mybir.dt.int32
+U32 = mybir.dt.uint32
+U16 = mybir.dt.uint16
+U8 = mybir.dt.uint8
+FP8X4 = mybir.dt.float8_e4m3fn_x4
+ALU = mybir.AluOpType
+ACT = mybir.ActivationFunctionType
+
+P = 128
+PACK = 4
+M = 128
+BLOCKS = J // M
+
+
+def tile_picked_zpq_soft_p_kernel(
+    tc, x_words, x_scales, e_words, e_scales, f_words, f_scales, hT, gT, rT, offs, code2, code3, out
+):
+    nc = tc.nc
+    words_in = (x_words, e_words, f_words)
+    scales_in = (x_scales, e_scales, f_scales)
+    queries = (hT, gT, rT)
+    lists_in = (offs, code2, code3)
+
+    with ExitStack() as ctx:
+        keep = ctx.enter_context(tc.tile_pool(name="keep", bufs=1))
+        psum = ctx.enter_context(tc.psum_pool(name="psum", bufs=1))
+
+        lists = [keep.tile([P, S // 16], U16, name="list%d" % a) for a in range(3)]
+        word_win = {}
+        byte_win = [keep.tile([P, T], U8, name="byte_win%d" % a, tag="slotb%d" % a, align_bytes=64) for a in range(3)]
+        picked_words = {}
+        picked_bytes = keep.tile([P, 3 * S], U8, name="picked_bytes", align_bytes=64)
+        planes = keep.tile([P, 3 * S], U8, name="planes", align_bytes=64)
+        warm = keep.tile([P, 2], F32, name="warm")
+
+        for a in range(3):
+            nc.scalar.dma_start(out=byte_win[a][112:P, :].bitcast(I32), in_=scales_in[a][0].bitcast(I32))
+        for a in range(3):
+            nc.vector.memset(byte_win[a][0:112, :].bitcast(I32), 0)
+        nc.vector.memset(warm[:, 0:1], 0.0)
+        nc.scalar.activation(out=warm[:, 1:2], in_=warm[:, 0:1], func=ACT.Exp)
+        nc.vector.memset(planes[:].bitcast(I32), 0)
+
+        late = []
+        late_at = [0]
+
+        def late_room(n):
+            if not late:
+                late.append(keep.tile([P, 5120], F32, name="late", tag="slot0", align_bytes=64))
+            at = late_at[0]
+            late_at[0] = at + n
+            return late[0][:, at : at + n]
+
+        def load_words(a):
+            word_win[a] = keep.tile([P, T], I32, name="word_win%d" % a, tag="slot%d" % a, align_bytes=64)
+            nc.sync.dma_start(out=word_win[a][:], in_=words_in[a][0].rearrange("p n t -> p (n t)").bitcast(I32))
+
+        raws = {}
+
+        def load_piece(part, b0, nb):
+            w = nb * M
+            if 0 in picked_words:
+                room = late_room(PACK * w)
+            else:
+                room = keep.tile([P, PACK * w], F32, name="early%d%d" % (part, b0), align_bytes=64)[:]
+            raw = room.rearrange("p (j c) -> p j c", j=PACK)
+            nc.sync.dma_start(out=raw, in_=queries[part][:, b0 * M : b0 * M + w].rearrange("(p j) c -> p j c", j=PACK))
+            for u in range(nb):
+                raws[(part, b0 + u)] = raw[:, :, u * M : (u + 1) * M]
+
+        nc.sync.dma_start(lists[0][:], lists_in[0])
+        nc.sync.dma_start(lists[1][:], lists_in[1])
+        nc.sync.dma_start(lists[2][:], lists_in[2])
+        load_words(0)
+        load_words(1)
+        load_piece(0, 0, 2)
+        load_words(2)
+
+        def gather_bytes(a):
+            nc.vector.tensor_copy(picked_bytes[:, a * S : (a + 1) * S], byte_win[a][:].indirect(lists[a][:]))
+
+        def gather_words(a):
+            picked_words[a] = keep.tile(
+                [P, S], U32, name="picked_words%d" % a, tag="slotb2" if a == 0 else "pw%d" % a, align_bytes=64
+            )
+            nc.vector.tensor_copy(picked_words[a][:], word_win[a][:].bitcast(U32).indirect(lists[a][:]))
+
+        def move_planes():
+            for r in range(4):
+                nc.scalar.dma_start(
+                    out=planes[r:P:32, :].bitcast(I32), in_=picked_bytes[112 + r : P : 4, :].bitcast(I32)
+                )
+
+        clk = keep.tile([P, 64], F32, name="clk")
+
+        def clock(ap, n):
+            nc.gpsimd.tensor_copy(out=clk[:, 8 * n : 8 * n + 1], in_=ap)
+
+        scores = [psum.tile([M, S], F32, name="scores%d" % b) for b in range(BLOCKS)]
+        grouped = {}
+        passes_done = [0] * BLOCKS
+
+        def cast(part, b, on):
+            g = keep.tile([P, M * PACK], BF16, name="grouped%d%d" % (part, b), align_bytes=64)
+            grouped[(part, b)] = g
+            src = raws[(part, b)].rearrange("p t (c i) -> p c t i", i=4)
+            dst = g[:].rearrange("p (c i t) -> p c t i", i=4, t=PACK)
+            if on == "v":
+                nc.vector.tensor_copy(out=dst, in_=src)
+            elif on == "s":
+                nc.scalar.copy(out=dst, in_=src)
+            else:
+                nc.scalar.copy(out=dst[:, 0:12], in_=src[:, 0:12])
+                nc.vector.tensor_copy(out=dst[:, 12:32], in_=src[:, 12:32])
+
+        def quantise_and_multiply(part, b):
+            codes = keep.tile([P, M], U32, name="codes%d%d" % (part, b), align_bytes=64)
+            scale = keep.tile([P, M], U8, name="scale%d%d" % (part, b), align_bytes=64)
+            nc.vector.quantize_mx(out=codes[:].bitcast(FP8X4), scales=scale[:], in_=grouped[(part, b)][:])
+            nc.tensor.matmul_mx(
+                out=scores[b][:],
+                lhsT=codes[:].bitcast(FP8X4),
+                lhsT_scale=scale[:],
+                rhs=picked_words[part][:].bitcast(FP8X4),
+                rhs_scale=planes[:, part * S : (part + 1) * S],
+                start=passes_done[b] == 0,
+                stop=passes_done[b] == 2,
+            )
+            passes_done[b] = passes_done[b] + 1
+
+        stats = [keep.tile([P, 24], F32, name="stats%d" % b) for b in range(BLOCKS)]
+        expd = [keep.tile([P, S], F32, name="expd%d" % b) for b in range(BLOCKS)]
+        result = [[keep.tile([P, S], F32, name="result%d_%d" % (b, h)) for h in range(2)] for b in range(BLOCKS)]
+
+        def row_max(b):
+            nc.vector.tensor_reduce(
+                out=stats[b][:, 0:1], in_=scores[b][:], axis=mybir.AxisListType.X, op=ALU.max, negate=True
+            )
+
+        def exponent(b):
+            nc.scalar.activation(
+                out=expd[b][:], in_=scores[b][:], func=ACT.Exp, bias=stats[b][:, 0:1], accum_out=stats[b][:, 8:9]
+            )
+
+        def invert(b):
+            nc.vector.reciprocal(out=stats[b][:, 16:17], in_=stats[b][:, 8:9])
+
+        def finish(b, on):
+            inv = stats[b][:, 16:17]
+            rows = slice(b * M, (b + 1) * M)
+            if on == "halves":
+                c = 320
+                nc.vector.tensor_scalar(out=result[b][0][:, 0:c], in0=expd[b][:, 0:c], scalar1=inv, scalar2=None, op0=ALU.mult)
+                nc.scalar.activation(out=result[b][1][:, c:S], in_=expd[b][:, c:S], func=ACT.Copy, scale=inv)
+                nc.sync.dma_start(out=out[rows, 0:c], in_=result[b][0][:, 0:c])
+                nc.scalar.dma_start(out=out[rows, c:S], in_=result[b][1][:, c:S])
+                return
+            if on == "v":
+                nc.vector.tensor_scalar(out=result[b][0][:], in0=expd[b][:], scalar1=inv, scalar2=None, op0=ALU.mult)
+            elif on == "s":
+                nc.scalar.activation(out=result[b][0][:], in_=expd[b][:], func=ACT.Copy, scale=inv)
+            else:
+                nc.gpsimd.tensor_scalar(
+                    out=result[b][0][:], in0=expd[b][:], scalar1=inv, scalar2=0.0, op0=ALU.mult, op1=ALU.add
+                )
+            nc.sync.dma_start(out=out[rows, :], in_=result[b][0][:])
+
+        for a in range(3):
+            gather_bytes(a)
+        move_planes()
+        gather_words(0)
+        load_piece(1, 0, 2)
+        load_piece(2, 0, 2)
+        load_piece(0, 2, 2)
+        load_piece(1, 2, 1)
+        load_piece(2, 2, 1)
+        load_piece(1, 3, 1)
+        load_piece(2, 3, 1)
+        gather_words(1)
+        cast(0, 0, "s")
+        cast(0, 1, "s")
+        quantise_and_multiply(0, 0)
+        quantise_and_multiply(0, 1)
+        gather_words(2)
+        cast(1, 0, "s")
+        cast(1, 1, "v")
+        quantise_and_multiply(1, 0)
+        quantise_and_multiply(1, 1)
+        cast(2, 0, "s")
+        cast(2, 1, "v")
+        quantise_and_multiply(2, 0)
+        quantise_and_multiply(2, 1)
+        cast(0, 2, "s")
+        cast(0, 3, "v")
+        row_max(0)
+        cast(1, 2, "s")
+        quantise_and_multiply(0, 2)
+        row_max(1)
+        cast(2, 2, "s")
+        quantise_and_multiply(0, 3)
+        exponent(0)
+        quantise_and_multiply(1, 2)
+        quantise_and_multiply(2, 2)
+        cast(1, 3, "v")
+        cast(2, 3, "s")
+        invert(0)
+        quantise_and_multiply(1, 3)
+        exponent(1)
+        quantise_and_multiply(2, 3)
+        row_max(2)
+        finish(0, "s")
+        invert(1)
+        row_max(3)
+        exponent(2)
+        finish(1, "v")
+        exponent(3)
+        invert(2)
+        finish(2, "v")
+        invert(3)
+        finish(3, "v")

@@ -55,13 +55,13 @@ def tile_picked_zpq_soft_p_kernel(
 
         def late_room(n):
             if not late:
-                late.append(keep.tile([P, 5120], F32, name="late", tag="slot0", align_bytes=64))
+                late.append(keep.tile([P, 2048], F32, name="late", tag="early00", align_bytes=64))
             at = late_at[0]
             late_at[0] = at + n
             return late[0][:, at : at + n]
 
         def load_words(a):
-            word_win[a] = keep.tile([P, T], I32, name="word_win%d" % a, tag="slot%d" % a, align_bytes=64)
+            word_win[a] = keep.tile([P, T], I32, name="word_win%d" % a, tag="slot%d" % (a % 2), align_bytes=64)
             nc.sync.dma_start(out=word_win[a][:], in_=words_in[a][0].rearrange("p n t -> p (n t)").bitcast(I32))
 
         raws = {}
@@ -71,7 +71,7 @@ def tile_picked_zpq_soft_p_kernel(
             if 0 in picked_words:
                 room = late_room(PACK * w)
             else:
-                room = keep.tile([P, PACK * w], F32, name="early%d%d" % (part, b0), align_bytes=64)[:]
+                room = keep.tile([P, PACK * w], F32, name="early%d%d" % (part, b0), tag="early%d%d" % (part, b0), align_bytes=64)[:]
             raw = room.rearrange("p (j c) -> p j c", j=PACK)
             nc.sync.dma_start(out=raw, in_=queries[part][:, b0 * M : b0 * M + w].rearrange("(p j) c -> p j c", j=PACK))
             for u in range(nb):
@@ -81,9 +81,9 @@ def tile_picked_zpq_soft_p_kernel(
         nc.sync.dma_start(lists[1][:], lists_in[1])
         nc.sync.dma_start(lists[2][:], lists_in[2])
         load_words(0)
+        load_piece(0, 0, 4)
         load_words(1)
-        load_piece(0, 0, 2)
-        load_words(2)
+        load_piece(1, 0, 4)
 
         def gather_bytes(a):
             nc.vector.tensor_copy(picked_bytes[:, a * S : (a + 1) * S], byte_win[a][:].indirect(lists[a][:]))
@@ -178,44 +178,42 @@ def tile_picked_zpq_soft_p_kernel(
             gather_bytes(a)
         move_planes()
         gather_words(0)
-        load_piece(1, 0, 2)
-        load_piece(2, 0, 2)
-        load_piece(0, 2, 2)
-        load_piece(1, 2, 1)
-        load_piece(2, 2, 1)
-        load_piece(1, 3, 1)
-        load_piece(2, 3, 1)
-        gather_words(1)
+        load_words(2)
         cast(0, 0, "s")
         cast(0, 1, "s")
         quantise_and_multiply(0, 0)
-        quantise_and_multiply(0, 1)
-        gather_words(2)
-        cast(1, 0, "s")
-        cast(1, 1, "v")
-        quantise_and_multiply(1, 0)
-        quantise_and_multiply(1, 1)
-        cast(2, 0, "s")
-        cast(2, 1, "v")
-        quantise_and_multiply(2, 0)
-        quantise_and_multiply(2, 1)
         cast(0, 2, "s")
-        cast(0, 3, "v")
-        row_max(0)
-        cast(1, 2, "s")
+        quantise_and_multiply(0, 1)
+        cast(0, 3, "s")
+        load_piece(2, 0, 1)
+        load_piece(2, 1, 1)
+        load_piece(2, 2, 1)
+        load_piece(2, 3, 1)
         quantise_and_multiply(0, 2)
-        row_max(1)
-        cast(2, 2, "s")
         quantise_and_multiply(0, 3)
-        exponent(0)
-        quantise_and_multiply(1, 2)
-        quantise_and_multiply(2, 2)
+        gather_words(1)
+        cast(1, 0, "s")
         cast(1, 3, "v")
-        cast(2, 3, "s")
-        invert(0)
+        cast(1, 1, "s")
+        quantise_and_multiply(1, 0)
         quantise_and_multiply(1, 3)
-        exponent(1)
+        cast(1, 2, "s")
+        quantise_and_multiply(1, 1)
+        quantise_and_multiply(1, 2)
+        gather_words(2)
+        cast(2, 0, "s")
+        quantise_and_multiply(2, 0)
+        cast(2, 1, "s")
+        quantise_and_multiply(2, 1)
+        cast(2, 2, "s")
+        row_max(0)
+        quantise_and_multiply(2, 2)
+        cast(2, 3, "s")
+        exponent(0)
+        row_max(1)
         quantise_and_multiply(2, 3)
+        invert(0)
+        exponent(1)
         row_max(2)
         finish(0, "s")
         invert(1)
@@ -226,4 +224,4 @@ def tile_picked_zpq_soft_p_kernel(
         invert(2)
         finish(2, "v")
         invert(3)
-        finish(3, "v")
+        finish(3, "halves")

@@ -55,13 +55,13 @@ def tile_picked_zpq_soft_p_kernel(
 
         def late_room(n):
             if not late:
-                late.append(keep.tile([P, 2048], F32, name="late", tag="early00", align_bytes=64))
+                late.append(keep.tile([P, 2048], F32, name="late", tag="slot0", align_bytes=64))
             at = late_at[0]
             late_at[0] = at + n
             return late[0][:, at : at + n]
 
         def load_words(a):
-            word_win[a] = keep.tile([P, T], I32, name="word_win%d" % a, tag="slot%d" % (a % 2), align_bytes=64)
+            word_win[a] = keep.tile([P, T], I32, name="word_win%d" % a, tag=("slot0", "slot1", "slotb2")[a], align_bytes=64)
             nc.sync.dma_start(out=word_win[a][:], in_=words_in[a][0].rearrange("p n t -> p (n t)").bitcast(I32))
 
         raws = {}
@@ -90,20 +90,15 @@ def tile_picked_zpq_soft_p_kernel(
 
         def gather_words(a):
             picked_words[a] = keep.tile(
-                [P, S], U32, name="picked_words%d" % a, tag="slotb2" if a == 0 else "pw%d" % a, align_bytes=64
+                [P, S], U32, name="picked_words%d" % a, tag="pw%d" % a, align_bytes=64
             )
             nc.vector.tensor_copy(picked_words[a][:], word_win[a][:].bitcast(U32).indirect(lists[a][:]))
 
         def move_planes():
             for r in range(4):
-                nc.scalar.dma_start(
+                nc.sync.dma_start(
                     out=planes[r:P:32, :].bitcast(I32), in_=picked_bytes[112 + r : P : 4, :].bitcast(I32)
                 )
-
-        clk = keep.tile([P, 64], F32, name="clk")
-
-        def clock(ap, n):
-            nc.gpsimd.tensor_copy(out=clk[:, 8 * n : 8 * n + 1], in_=ap)
 
         scores = [psum.tile([M, S], F32, name="scores%d" % b) for b in range(BLOCKS)]
         grouped = {}
@@ -177,8 +172,8 @@ def tile_picked_zpq_soft_p_kernel(
         for a in range(3):
             gather_bytes(a)
         move_planes()
-        gather_words(0)
         load_words(2)
+        gather_words(0)
         cast(0, 0, "s")
         cast(0, 1, "s")
         quantise_and_multiply(0, 0)

@@ -210,7 +210,7 @@ def tile_picked_zpq_soft_p_kernel(
         invert(0)
         exponent(1)
         row_max(2)
-        finish(0, "s")
+        finish(0, "g")
         invert(1)
         row_max(3)
         exponent(2)

@@ -40,14 +40,11 @@ def tile_picked_zpq_soft_p_kernel(
         picked_words = {}
         picked_bytes = keep.tile([P, 3 * S], U8, name="picked_bytes", align_bytes=64)
         planes = keep.tile([P, 3 * S], U8, name="planes", align_bytes=64)
-        warm = keep.tile([P, 2], F32, name="warm")
 
         for a in range(3):
             nc.scalar.dma_start(out=byte_win[a][112:P, :].bitcast(I32), in_=scales_in[a][0].bitcast(I32))
         for a in range(3):
             nc.vector.memset(byte_win[a][0:112, :].bitcast(I32), 0)
-        nc.vector.memset(warm[:, 0:1], 0.0)
-        nc.scalar.activation(out=warm[:, 1:2], in_=warm[:, 0:1], func=ACT.Exp)
         nc.vector.memset(planes[:].bitcast(I32), 0)
 
         late = []
@@ -112,7 +109,7 @@ def tile_picked_zpq_soft_p_kernel(
             if on == "v":
                 nc.vector.tensor_copy(out=dst, in_=src)
             elif on == "s":
-                nc.scalar.copy(out=dst, in_=src)
+                nc.scalar.activation(out=dst, in_=src, func=ACT.Copy)
             else:
                 nc.scalar.copy(out=dst[:, 0:12], in_=src[:, 0:12])
                 nc.vector.tensor_copy(out=dst[:, 12:32], in_=src[:, 12:32])

@@ -18,7 +18,15 @@ ACT = mybir.ActivationFunctionType
 P = 128
 PACK = 4
 M = 128
-BLOCKS = J // M
+TILES = J // M
+PARTS = 3
+LAST = PARTS - 1
+SCALE_ROWS = K // 32
+SCALES_AT = P - SCALE_ROWS
+QUAD = 32
+RUN = 4
+VECTOR_SHARE = 320
+NEG_MAX, ROW_SUM, INVERSE, STATS = 0, 8, 16, 24
 
 
 def tile_picked_zpq_soft_p_kernel(
@@ -34,186 +42,119 @@ def tile_picked_zpq_soft_p_kernel(
         keep = ctx.enter_context(tc.tile_pool(name="keep", bufs=1))
         psum = ctx.enter_context(tc.psum_pool(name="psum", bufs=1))
 
-        lists = [keep.tile([P, S // 16], U16, name="list%d" % a) for a in range(3)]
-        word_win = {}
-        byte_win = [keep.tile([P, T], U8, name="byte_win%d" % a, tag="slotb%d" % a, align_bytes=64) for a in range(3)]
+        after_bytes = "last scale table, then last word table"
+        after_words = "first word table, then last queries"
+
+        lists = [keep.tile([P, S // 16], U16, name="list%d" % a) for a in range(PARTS)]
+        byte_tags = ["byte_window0", "byte_window1", after_bytes]
+        byte_window = [
+            keep.tile([P, T], U8, name="byte_window%d" % a, tag=byte_tags[a], align_bytes=64) for a in range(PARTS)
+        ]
+        picked_bytes = keep.tile([P, PARTS * S], U8, name="picked_bytes", align_bytes=64)
+        moving_scales = keep.tile([P, PARTS * S], U8, name="moving_scales", align_bytes=64)
+
+        for a in range(PARTS):
+            nc.scalar.dma_start(out=byte_window[a][SCALES_AT:P, :].bitcast(I32), in_=scales_in[a][0].bitcast(I32))
+        for a in range(PARTS):
+            nc.vector.memset(byte_window[a][0:SCALES_AT, :].bitcast(I32), 0)
+        nc.vector.memset(moving_scales[:].bitcast(I32), 0)
+
+        word_window = {}
+        raw = {}
+
+        def load_words(a, tag):
+            word_window[a] = keep.tile([P, T], I32, name="word_window%d" % a, tag=tag, align_bytes=64)
+            nc.sync.dma_start(out=word_window[a][:], in_=words_in[a][0].rearrange("p n t -> p (n t)").bitcast(I32))
+
+        def load_queries(part, first_tile, tiles, room):
+            rows = room.rearrange("p (t c) -> p t c", t=PACK)
+            columns = queries[part][:, first_tile * M : (first_tile + tiles) * M]
+            nc.sync.dma_start(out=rows, in_=columns.rearrange("(p t) c -> p t c", t=PACK))
+            for u in range(tiles):
+                raw[(part, first_tile + u)] = rows[:, :, u * M : (u + 1) * M]
+
         picked_words = {}
-        picked_bytes = keep.tile([P, 3 * S], U8, name="picked_bytes", align_bytes=64)
-        planes = keep.tile([P, 3 * S], U8, name="planes", align_bytes=64)
-
-        for a in range(3):
-            nc.scalar.dma_start(out=byte_win[a][112:P, :].bitcast(I32), in_=scales_in[a][0].bitcast(I32))
-        for a in range(3):
-            nc.vector.memset(byte_win[a][0:112, :].bitcast(I32), 0)
-        nc.vector.memset(planes[:].bitcast(I32), 0)
-
-        late = []
-        late_at = [0]
-
-        def late_room(n):
-            if not late:
-                late.append(keep.tile([P, 2048], F32, name="late", tag="slot0", align_bytes=64))
-            at = late_at[0]
-            late_at[0] = at + n
-            return late[0][:, at : at + n]
-
-        def load_words(a):
-            word_win[a] = keep.tile([P, T], I32, name="word_win%d" % a, tag=("slot0", "slot1", "slotb2")[a], align_bytes=64)
-            nc.sync.dma_start(out=word_win[a][:], in_=words_in[a][0].rearrange("p n t -> p (n t)").bitcast(I32))
-
-        raws = {}
-
-        def load_piece(part, b0, nb):
-            w = nb * M
-            if 0 in picked_words:
-                room = late_room(PACK * w)
-            else:
-                room = keep.tile([P, PACK * w], F32, name="early%d%d" % (part, b0), tag="early%d%d" % (part, b0), align_bytes=64)[:]
-            raw = room.rearrange("p (j c) -> p j c", j=PACK)
-            nc.sync.dma_start(out=raw, in_=queries[part][:, b0 * M : b0 * M + w].rearrange("(p j) c -> p j c", j=PACK))
-            for u in range(nb):
-                raws[(part, b0 + u)] = raw[:, :, u * M : (u + 1) * M]
-
-        nc.sync.dma_start(lists[0][:], lists_in[0])
-        nc.sync.dma_start(lists[1][:], lists_in[1])
-        nc.sync.dma_start(lists[2][:], lists_in[2])
-        load_words(0)
-        load_piece(0, 0, 4)
-        load_words(1)
-        load_piece(1, 0, 4)
-
-        def gather_bytes(a):
-            nc.vector.tensor_copy(picked_bytes[:, a * S : (a + 1) * S], byte_win[a][:].indirect(lists[a][:]))
 
         def gather_words(a):
-            picked_words[a] = keep.tile(
-                [P, S], U32, name="picked_words%d" % a, tag="pw%d" % a, align_bytes=64
+            picked_words[a] = keep.tile([P, S], U32, name="picked_words%d" % a, align_bytes=64)
+            nc.vector.tensor_copy(picked_words[a][:], word_window[a][:].bitcast(U32).indirect(lists[a][:]))
+
+        for a in range(PARTS):
+            nc.sync.dma_start(lists[a][:], lists_in[a])
+        word_tags = [after_words, "word_window1"]
+        for a in range(LAST):
+            load_words(a, word_tags[a])
+            whole = keep.tile([P, PACK * J], F32, name="queries%d" % a, align_bytes=64)
+            load_queries(a, 0, TILES, whole[:])
+
+        for a in range(PARTS):
+            nc.vector.tensor_copy(picked_bytes[:, a * S : (a + 1) * S], byte_window[a][:].indirect(lists[a][:]))
+        for r in range(PACK):
+            nc.sync.dma_start(
+                out=moving_scales[r:P:QUAD, :].bitcast(I32), in_=picked_bytes[SCALES_AT + r : P : PACK, :].bitcast(I32)
             )
-            nc.vector.tensor_copy(picked_words[a][:], word_win[a][:].bitcast(U32).indirect(lists[a][:]))
 
-        def move_planes():
-            for r in range(4):
-                nc.sync.dma_start(
-                    out=planes[r:P:32, :].bitcast(I32), in_=picked_bytes[112 + r : P : 4, :].bitcast(I32)
-                )
+        load_words(LAST, after_bytes)
+        gather_words(0)
+        last_queries = keep.tile([P, PACK * J], F32, name="last_queries", tag=after_words, align_bytes=64)
+        for b in range(TILES):
+            load_queries(LAST, b, 1, last_queries[:, b * PACK * M : (b + 1) * PACK * M])
 
-        scores = [psum.tile([M, S], F32, name="scores%d" % b) for b in range(BLOCKS)]
-        grouped = {}
-        passes_done = [0] * BLOCKS
+        scores = [psum.tile([M, S], F32, name="scores%d" % b) for b in range(TILES)]
 
-        def cast(part, b, on):
-            g = keep.tile([P, M * PACK], BF16, name="grouped%d%d" % (part, b), align_bytes=64)
-            grouped[(part, b)] = g
-            src = raws[(part, b)].rearrange("p t (c i) -> p c t i", i=4)
-            dst = g[:].rearrange("p (c i t) -> p c t i", i=4, t=PACK)
-            if on == "v":
+        def multiply(part, b):
+            grouped = keep.tile([P, M * PACK], BF16, name="grouped%d%d" % (part, b), align_bytes=64)
+            src = raw[(part, b)].rearrange("p t (c i) -> p c t i", i=RUN)
+            dst = grouped[:].rearrange("p (c i t) -> p c t i", i=RUN, t=PACK)
+            if (part, b) == (LAST - 1, TILES - 1):
                 nc.vector.tensor_copy(out=dst, in_=src)
-            elif on == "s":
-                nc.scalar.activation(out=dst, in_=src, func=ACT.Copy)
             else:
-                nc.scalar.copy(out=dst[:, 0:12], in_=src[:, 0:12])
-                nc.vector.tensor_copy(out=dst[:, 12:32], in_=src[:, 12:32])
-
-        def quantise_and_multiply(part, b):
+                nc.scalar.activation(out=dst, in_=src, func=ACT.Copy)
             codes = keep.tile([P, M], U32, name="codes%d%d" % (part, b), align_bytes=64)
-            scale = keep.tile([P, M], U8, name="scale%d%d" % (part, b), align_bytes=64)
-            nc.vector.quantize_mx(out=codes[:].bitcast(FP8X4), scales=scale[:], in_=grouped[(part, b)][:])
+            scales = keep.tile([P, M], U8, name="scales%d%d" % (part, b), align_bytes=64)
+            nc.vector.quantize_mx(out=codes[:].bitcast(FP8X4), scales=scales[:], in_=grouped[:])
             nc.tensor.matmul_mx(
                 out=scores[b][:],
                 lhsT=codes[:].bitcast(FP8X4),
-                lhsT_scale=scale[:],
+                lhsT_scale=scales[:],
                 rhs=picked_words[part][:].bitcast(FP8X4),
-                rhs_scale=planes[:, part * S : (part + 1) * S],
-                start=passes_done[b] == 0,
-                stop=passes_done[b] == 2,
-            )
-            passes_done[b] = passes_done[b] + 1
-
-        stats = [keep.tile([P, 24], F32, name="stats%d" % b) for b in range(BLOCKS)]
-        expd = [keep.tile([P, S], F32, name="expd%d" % b) for b in range(BLOCKS)]
-        result = [[keep.tile([P, S], F32, name="result%d_%d" % (b, h)) for h in range(2)] for b in range(BLOCKS)]
-
-        def row_max(b):
-            nc.vector.tensor_reduce(
-                out=stats[b][:, 0:1], in_=scores[b][:], axis=mybir.AxisListType.X, op=ALU.max, negate=True
+                rhs_scale=moving_scales[:, part * S : (part + 1) * S],
+                start=part == 0,
+                stop=part == LAST,
             )
 
-        def exponent(b):
-            nc.scalar.activation(
-                out=expd[b][:], in_=scores[b][:], func=ACT.Exp, bias=stats[b][:, 0:1], accum_out=stats[b][:, 8:9]
-            )
+        for part in range(PARTS):
+            if part > 0:
+                gather_words(part)
+            for b in range(TILES):
+                multiply(part, b)
 
-        def invert(b):
-            nc.vector.reciprocal(out=stats[b][:, 16:17], in_=stats[b][:, 8:9])
+        for b in range(TILES):
+            stats = keep.tile([P, STATS], F32, name="stats%d" % b)
+            neg_max = stats[:, NEG_MAX : NEG_MAX + 1]
+            row_sum = stats[:, ROW_SUM : ROW_SUM + 1]
+            inverse = stats[:, INVERSE : INVERSE + 1]
+            powers = keep.tile([P, S], F32, name="powers%d" % b)
+            nc.vector.tensor_reduce(out=neg_max, in_=scores[b][:], axis=mybir.AxisListType.X, op=ALU.max, negate=True)
+            nc.scalar.activation(out=powers[:], in_=scores[b][:], func=ACT.Exp, bias=neg_max, accum_out=row_sum)
+            nc.vector.reciprocal(out=inverse, in_=row_sum)
 
-        def finish(b, on):
-            inv = stats[b][:, 16:17]
             rows = slice(b * M, (b + 1) * M)
-            if on == "halves":
-                c = 320
-                nc.vector.tensor_scalar(out=result[b][0][:, 0:c], in0=expd[b][:, 0:c], scalar1=inv, scalar2=None, op0=ALU.mult)
-                nc.scalar.activation(out=result[b][1][:, c:S], in_=expd[b][:, c:S], func=ACT.Copy, scale=inv)
-                nc.sync.dma_start(out=out[rows, 0:c], in_=result[b][0][:, 0:c])
-                nc.scalar.dma_start(out=out[rows, c:S], in_=result[b][1][:, c:S])
-                return
-            if on == "v":
-                nc.vector.tensor_scalar(out=result[b][0][:], in0=expd[b][:], scalar1=inv, scalar2=None, op0=ALU.mult)
-            elif on == "s":
-                nc.scalar.activation(out=result[b][0][:], in_=expd[b][:], func=ACT.Copy, scale=inv)
-            else:
+            result = keep.tile([P, S], F32, name="result%d" % b)
+            if b == 0:
                 nc.gpsimd.tensor_scalar(
-                    out=result[b][0][:], in0=expd[b][:], scalar1=inv, scalar2=0.0, op0=ALU.mult, op1=ALU.add
+                    out=result[:], in0=powers[:], scalar1=inverse, scalar2=0.0, op0=ALU.mult, op1=ALU.add
                 )
-            nc.sync.dma_start(out=out[rows, :], in_=result[b][0][:])
-
-        for a in range(3):
-            gather_bytes(a)
-        move_planes()
-        load_words(2)
-        gather_words(0)
-        cast(0, 0, "s")
-        cast(0, 1, "s")
-        quantise_and_multiply(0, 0)
-        cast(0, 2, "s")
-        quantise_and_multiply(0, 1)
-        cast(0, 3, "s")
-        load_piece(2, 0, 1)
-        load_piece(2, 1, 1)
-        load_piece(2, 2, 1)
-        load_piece(2, 3, 1)
-        quantise_and_multiply(0, 2)
-        quantise_and_multiply(0, 3)
-        gather_words(1)
-        cast(1, 0, "s")
-        cast(1, 3, "v")
-        cast(1, 1, "s")
-        quantise_and_multiply(1, 0)
-        quantise_and_multiply(1, 3)
-        cast(1, 2, "s")
-        quantise_and_multiply(1, 1)
-        quantise_and_multiply(1, 2)
-        gather_words(2)
-        cast(2, 0, "s")
-        quantise_and_multiply(2, 0)
-        cast(2, 1, "s")
-        quantise_and_multiply(2, 1)
-        cast(2, 2, "s")
-        row_max(0)
-        quantise_and_multiply(2, 2)
-        cast(2, 3, "s")
-        exponent(0)
-        row_max(1)
-        quantise_and_multiply(2, 3)
-        invert(0)
-        exponent(1)
-        row_max(2)
-        finish(0, "g")
-        invert(1)
-        row_max(3)
-        exponent(2)
-        finish(1, "v")
-        exponent(3)
-        invert(2)
-        finish(2, "v")
-        invert(3)
-        finish(3, "halves")
+                nc.sync.dma_start(out=out[rows, :], in_=result[:])
+            elif b < TILES - 1:
+                nc.vector.tensor_scalar(out=result[:], in0=powers[:], scalar1=inverse, scalar2=None, op0=ALU.mult)
+                nc.sync.dma_start(out=out[rows, :], in_=result[:])
+            else:
+                left, right = slice(0, VECTOR_SHARE), slice(VECTOR_SHARE, S)
+                rest = keep.tile([P, S], F32, name="result_rest")
+                nc.vector.tensor_scalar(
+                    out=result[:, left], in0=powers[:, left], scalar1=inverse, scalar2=None, op0=ALU.mult
+                )
+                nc.scalar.activation(out=rest[:, right], in_=powers[:, right], func=ACT.Copy, scale=inverse)
+                nc.sync.dma_start(out=out[rows, left], in_=result[:, left])
+                nc.scalar.dma_start(out=out[rows, right], in_=rest[:, right])

@@ -102,16 +102,20 @@ def tile_picked_zpq_soft_p_kernel(
 
         scores = [psum.tile([M, S], F32, name="scores%d" % b) for b in range(TILES)]
 
-        def multiply(part, b):
+        def multiply(part, b, scale_tag=None):
             grouped = keep.tile([P, M * PACK], BF16, name="grouped%d%d" % (part, b), align_bytes=64)
             src = raw[(part, b)].rearrange("p t (c i) -> p c t i", i=RUN)
             dst = grouped[:].rearrange("p (c i t) -> p c t i", i=RUN, t=PACK)
             if (part, b) == (LAST - 1, TILES - 1):
                 nc.vector.tensor_copy(out=dst, in_=src)
+            elif (part, b) == (LAST, TILES - 1):
+                nc.gpsimd.tensor_scalar(out=dst, in0=src, scalar1=1.0, scalar2=0.0, op0=ALU.mult, op1=ALU.add)
             else:
                 nc.scalar.activation(out=dst, in_=src, func=ACT.Copy)
             codes = keep.tile([P, M], U32, name="codes%d%d" % (part, b), align_bytes=64)
-            scales = keep.tile([P, M], U8, name="scales%d%d" % (part, b), align_bytes=64)
+            scales = keep.tile(
+                [P, M], U8, name="scales%d%d" % (part, b), tag=scale_tag or "scales%d%d" % (part, b), align_bytes=64
+            )
             nc.vector.quantize_mx(out=codes[:].bitcast(FP8X4), scales=scales[:], in_=grouped[:])
             nc.tensor.matmul_mx(
                 out=scores[b][:],
@@ -123,38 +127,48 @@ def tile_picked_zpq_soft_p_kernel(
                 stop=part == LAST,
             )
 
-        for part in range(PARTS):
-            if part > 0:
-                gather_words(part)
-            for b in range(TILES):
-                multiply(part, b)
+        powers = {}
+        stats = {}
 
-        for b in range(TILES):
-            stats = keep.tile([P, STATS], F32, name="stats%d" % b)
-            neg_max = stats[:, NEG_MAX : NEG_MAX + 1]
-            row_sum = stats[:, ROW_SUM : ROW_SUM + 1]
-            inverse = stats[:, INVERSE : INVERSE + 1]
-            powers = keep.tile([P, S], F32, name="powers%d" % b)
-            nc.vector.tensor_reduce(out=neg_max, in_=scores[b][:], axis=mybir.AxisListType.X, op=ALU.max, negate=True)
-            nc.scalar.activation(out=powers[:], in_=scores[b][:], func=ACT.Exp, bias=neg_max, accum_out=row_sum)
-            nc.vector.reciprocal(out=inverse, in_=row_sum)
+        def exponents(b, max_tag):
+            neg_max = keep.tile([P, 1], F32, name="neg_max%d" % b, tag=max_tag, align_bytes=64)
+            stats[b] = keep.tile([P, STATS], F32, name="stats%d" % b)
+            powers[b] = keep.tile([P, S], F32, name="powers%d" % b)
+            nc.vector.tensor_reduce(out=neg_max[:], in_=scores[b][:], axis=mybir.AxisListType.X, op=ALU.max, negate=True)
+            row_sum = stats[b][:, ROW_SUM : ROW_SUM + 1]
+            nc.scalar.activation(out=powers[b][:], in_=scores[b][:], func=ACT.Exp, bias=neg_max[:], accum_out=row_sum)
 
+        def normalise(b):
+            inverse = stats[b][:, INVERSE : INVERSE + 1]
+            nc.vector.reciprocal(out=inverse, in_=stats[b][:, ROW_SUM : ROW_SUM + 1])
             rows = slice(b * M, (b + 1) * M)
             result = keep.tile([P, S], F32, name="result%d" % b)
-            if b == 0:
+            if b < 1:
                 nc.gpsimd.tensor_scalar(
-                    out=result[:], in0=powers[:], scalar1=inverse, scalar2=0.0, op0=ALU.mult, op1=ALU.add
+                    out=result[:], in0=powers[b][:], scalar1=inverse, scalar2=0.0, op0=ALU.mult, op1=ALU.add
                 )
                 nc.sync.dma_start(out=out[rows, :], in_=result[:])
             elif b < TILES - 1:
-                nc.vector.tensor_scalar(out=result[:], in0=powers[:], scalar1=inverse, scalar2=None, op0=ALU.mult)
+                nc.vector.tensor_scalar(out=result[:], in0=powers[b][:], scalar1=inverse, scalar2=None, op0=ALU.mult)
                 nc.sync.dma_start(out=out[rows, :], in_=result[:])
             else:
                 left, right = slice(0, VECTOR_SHARE), slice(VECTOR_SHARE, S)
                 rest = keep.tile([P, S], F32, name="result_rest")
                 nc.vector.tensor_scalar(
-                    out=result[:, left], in0=powers[:, left], scalar1=inverse, scalar2=None, op0=ALU.mult
+                    out=result[:, left], in0=powers[b][:, left], scalar1=inverse, scalar2=None, op0=ALU.mult
                 )
-                nc.scalar.activation(out=rest[:, right], in_=powers[:, right], func=ACT.Copy, scale=inverse)
+                nc.scalar.activation(out=rest[:, right], in_=powers[b][:, right], func=ACT.Copy, scale=inverse)
                 nc.sync.dma_start(out=out[rows, left], in_=result[:, left])
                 nc.scalar.dma_start(out=out[rows, right], in_=rest[:, right])
+
+        for part in range(LAST):
+            if part > 0:
+                gather_words(part)
+            for b in range(TILES):
+                multiply(part, b)
+        gather_words(LAST)
+        for b in range(TILES):
+            multiply(LAST, b, "last two scale planes" if b >= TILES - 2 else None)
+        for b in range(TILES):
+            exponents(b, "neg_max%d" % (b % 2))
+            normalise(b)

@@ -40,6 +40,7 @@ def tile_picked_zpq_soft_p_kernel(
 
     with ExitStack() as ctx:
         keep = ctx.enter_context(tc.tile_pool(name="keep", bufs=1))
+        shared = ctx.enter_context(tc.tile_pool(name="shared", bufs=1))
         psum = ctx.enter_context(tc.psum_pool(name="psum", bufs=1))
 
         after_bytes = "last scale table, then last word table"
@@ -102,7 +103,7 @@ def tile_picked_zpq_soft_p_kernel(
 
         scores = [psum.tile([M, S], F32, name="scores%d" % b) for b in range(TILES)]
 
-        def multiply(part, b, scale_tag=None):
+        def multiply(part, b):
             grouped = keep.tile([P, M * PACK], BF16, name="grouped%d%d" % (part, b), align_bytes=64)
             src = raw[(part, b)].rearrange("p t (c i) -> p c t i", i=RUN)
             dst = grouped[:].rearrange("p (c i t) -> p c t i", i=RUN, t=PACK)
@@ -113,9 +114,10 @@ def tile_picked_zpq_soft_p_kernel(
             else:
                 nc.scalar.activation(out=dst, in_=src, func=ACT.Copy)
             codes = keep.tile([P, M], U32, name="codes%d%d" % (part, b), align_bytes=64)
-            scales = keep.tile(
-                [P, M], U8, name="scales%d%d" % (part, b), tag=scale_tag or "scales%d%d" % (part, b), align_bytes=64
-            )
+            if (part, b) == (LAST, TILES - 1):
+                scales = shared.tile([P, M], U8, name="last_scales", offset=64, align_bytes=64)
+            else:
+                scales = keep.tile([P, M], U8, name="scales%d%d" % (part, b), align_bytes=64)
             nc.vector.quantize_mx(out=codes[:].bitcast(FP8X4), scales=scales[:], in_=grouped[:])
             nc.tensor.matmul_mx(
                 out=scores[b][:],
@@ -130,20 +132,25 @@ def tile_picked_zpq_soft_p_kernel(
         powers = {}
         stats = {}
 
-        def exponents(b, max_tag):
-            neg_max = keep.tile([P, 1], F32, name="neg_max%d" % b, tag=max_tag, align_bytes=64)
+        def exponents(b):
+            if b == 0:
+                neg_max = shared.tile([P, 32], F32, name="neg_max0", offset=0)[:, 0:1]
+            elif b == 2:
+                neg_max = shared.tile([P, 1], F32, name="neg_max2", offset=0)[:]
+            else:
+                neg_max = keep.tile([P, 1], F32, name="neg_max%d" % b, tag="odd maxima")[:]
             stats[b] = keep.tile([P, STATS], F32, name="stats%d" % b)
             powers[b] = keep.tile([P, S], F32, name="powers%d" % b)
-            nc.vector.tensor_reduce(out=neg_max[:], in_=scores[b][:], axis=mybir.AxisListType.X, op=ALU.max, negate=True)
+            nc.vector.tensor_reduce(out=neg_max, in_=scores[b][:], axis=mybir.AxisListType.X, op=ALU.max, negate=True)
             row_sum = stats[b][:, ROW_SUM : ROW_SUM + 1]
-            nc.scalar.activation(out=powers[b][:], in_=scores[b][:], func=ACT.Exp, bias=neg_max[:], accum_out=row_sum)
+            nc.scalar.activation(out=powers[b][:], in_=scores[b][:], func=ACT.Exp, bias=neg_max, accum_out=row_sum)
 
         def normalise(b):
             inverse = stats[b][:, INVERSE : INVERSE + 1]
             nc.vector.reciprocal(out=inverse, in_=stats[b][:, ROW_SUM : ROW_SUM + 1])
             rows = slice(b * M, (b + 1) * M)
             result = keep.tile([P, S], F32, name="result%d" % b)
-            if b < 1:
+            if b < 2:
                 nc.gpsimd.tensor_scalar(
                     out=result[:], in0=powers[b][:], scalar1=inverse, scalar2=0.0, op0=ALU.mult, op1=ALU.add
                 )
@@ -167,8 +174,11 @@ def tile_picked_zpq_soft_p_kernel(
             for b in range(TILES):
                 multiply(part, b)
         gather_words(LAST)
-        for b in range(TILES):
-            multiply(LAST, b, "last two scale planes" if b >= TILES - 2 else None)
-        for b in range(TILES):
-            exponents(b, "neg_max%d" % (b % 2))
+        for b in range(TILES - 1):
+            multiply(LAST, b)
+        exponents(0)
+        normalise(0)
+        multiply(LAST, TILES - 1)
+        for b in range(1, TILES):
+            exponents(b)
             normalise(b)

@@ -24,8 +24,9 @@ LAST = PARTS - 1
 SCALE_ROWS = K // 32
 SCALES_AT = P - SCALE_ROWS
 QUAD = 32
+WIDE = 256
 RUN = 4
-VECTOR_SHARE = 320
+VECTOR_SHARE = 256
 NEG_MAX, ROW_SUM, INVERSE, STATS = 0, 8, 16, 24
 
 
@@ -49,10 +50,10 @@ def tile_picked_zpq_soft_p_kernel(
         lists = [keep.tile([P, S // 16], U16, name="list%d" % a) for a in range(PARTS)]
         byte_tags = ["byte_window0", "byte_window1", after_bytes]
         byte_window = [
-            keep.tile([P, T], U8, name="byte_window%d" % a, tag=byte_tags[a], align_bytes=64) for a in range(PARTS)
+            keep.tile([P, T], U8, name="byte_window%d" % a, tag=byte_tags[a], align_bytes=WIDE) for a in range(PARTS)
         ]
-        picked_bytes = keep.tile([P, PARTS * S], U8, name="picked_bytes", align_bytes=64)
-        moving_scales = keep.tile([P, PARTS * S], U8, name="moving_scales", align_bytes=64)
+        picked_bytes = keep.tile([P, PARTS * S], U8, name="picked_bytes", align_bytes=WIDE)
+        moving_scales = keep.tile([P, PARTS * S], U8, name="moving_scales", align_bytes=WIDE)
 
         for a in range(PARTS):
             nc.scalar.dma_start(out=byte_window[a][SCALES_AT:P, :].bitcast(I32), in_=scales_in[a][0].bitcast(I32))
@@ -64,7 +65,7 @@ def tile_picked_zpq_soft_p_kernel(
         raw = {}
 
         def load_words(a, tag):
-            word_window[a] = keep.tile([P, T], I32, name="word_window%d" % a, tag=tag, align_bytes=64)
+            word_window[a] = keep.tile([P, T], I32, name="word_window%d" % a, tag=tag, align_bytes=WIDE)
             nc.sync.dma_start(out=word_window[a][:], in_=words_in[a][0].rearrange("p n t -> p (n t)").bitcast(I32))
 
         def load_queries(part, first_tile, tiles, room):
@@ -77,7 +78,7 @@ def tile_picked_zpq_soft_p_kernel(
         picked_words = {}
 
         def gather_words(a):
-            picked_words[a] = keep.tile([P, S], U32, name="picked_words%d" % a, align_bytes=64)
+            picked_words[a] = keep.tile([P, S], U32, name="picked_words%d" % a, align_bytes=WIDE)
             nc.vector.tensor_copy(picked_words[a][:], word_window[a][:].bitcast(U32).indirect(lists[a][:]))
 
         for a in range(PARTS):
@@ -85,7 +86,7 @@ def tile_picked_zpq_soft_p_kernel(
         word_tags = [after_words, "word_window1"]
         for a in range(LAST):
             load_words(a, word_tags[a])
-            whole = keep.tile([P, PACK * J], F32, name="queries%d" % a, align_bytes=64)
+            whole = keep.tile([P, PACK * J], F32, name="queries%d" % a, align_bytes=WIDE)
             load_queries(a, 0, TILES, whole[:])
 
         for a in range(PARTS):
@@ -97,7 +98,7 @@ def tile_picked_zpq_soft_p_kernel(
 
         load_words(LAST, after_bytes)
         gather_words(0)
-        last_queries = keep.tile([P, PACK * J], F32, name="last_queries", tag=after_words, align_bytes=64)
+        last_queries = keep.tile([P, PACK * J], F32, name="last_queries", tag=after_words, align_bytes=WIDE)
         for b in range(TILES):
             load_queries(LAST, b, 1, last_queries[:, b * PACK * M : (b + 1) * PACK * M])
 
@@ -110,6 +111,8 @@ def tile_picked_zpq_soft_p_kernel(
             if (part, b) == (LAST - 1, TILES - 1):
                 nc.vector.tensor_copy(out=dst, in_=src)
             elif (part, b) == (LAST, TILES - 1):
+                src = raw[(part, b)].rearrange("p t c -> p c t")
+                dst = grouped[:].rearrange("p (c t) -> p c t", t=PACK)
                 nc.gpsimd.tensor_scalar(out=dst, in0=src, scalar1=1.0, scalar2=0.0, op0=ALU.mult, op1=ALU.add)
             else:
                 nc.scalar.activation(out=dst, in_=src, func=ACT.Copy)
@@ -140,7 +143,7 @@ def tile_picked_zpq_soft_p_kernel(
             else:
                 neg_max = keep.tile([P, 1], F32, name="neg_max%d" % b, tag="odd maxima")[:]
             stats[b] = keep.tile([P, STATS], F32, name="stats%d" % b)
-            powers[b] = keep.tile([P, S], F32, name="powers%d" % b)
+            powers[b] = keep.tile([P, S], F32, name="powers%d" % b, align_bytes=WIDE)
             nc.vector.tensor_reduce(out=neg_max, in_=scores[b][:], axis=mybir.AxisListType.X, op=ALU.max, negate=True)
             row_sum = stats[b][:, ROW_SUM : ROW_SUM + 1]
             nc.scalar.activation(out=powers[b][:], in_=scores[b][:], func=ACT.Exp, bias=neg_max, accum_out=row_sum)
@@ -149,7 +152,7 @@ def tile_picked_zpq_soft_p_kernel(
             inverse = stats[b][:, INVERSE : INVERSE + 1]
             nc.vector.reciprocal(out=inverse, in_=stats[b][:, ROW_SUM : ROW_SUM + 1])
             rows = slice(b * M, (b + 1) * M)
-            result = keep.tile([P, S], F32, name="result%d" % b)
+            result = keep.tile([P, S], F32, name="result%d" % b, align_bytes=WIDE)
             if b < 2:
                 nc.gpsimd.tensor_scalar(
                     out=result[:], in0=powers[b][:], scalar1=inverse, scalar2=0.0, op0=ALU.mult, op1=ALU.add
@@ -160,7 +163,7 @@ def tile_picked_zpq_soft_p_kernel(
                 nc.sync.dma_start(out=out[rows, :], in_=result[:])
             else:
                 left, right = slice(0, VECTOR_SHARE), slice(VECTOR_SHARE, S)
-                rest = keep.tile([P, S], F32, name="result_rest")
+                rest = keep.tile([P, S], F32, name="result_rest", align_bytes=WIDE)
                 nc.vector.tensor_scalar(
                     out=result[:, left], in0=powers[b][:, left], scalar1=inverse, scalar2=None, op0=ALU.mult
                 )

from contextlib import ExitStack

import concourse.mybir as mybir

K, T, S, J = 512, 2048, 512, 512
FLOPS = 2 * 3 * K * S * J

F32 = mybir.dt.float32
BF16 = mybir.dt.bfloat16
I32 = mybir.dt.int32
U32 = mybir.dt.uint32
U16 = mybir.dt.uint16
U8 = mybir.dt.uint8
FP8X4 = mybir.dt.float8_e4m3fn_x4
ALU = mybir.AluOpType
ACT = mybir.ActivationFunctionType

P = 128
PACK = 4
M = 128
TILES = J // M
PARTS = 3
LAST = PARTS - 1
SCALE_ROWS = K // 32
SCALES_AT = P - SCALE_ROWS
QUAD = 32
WIDE = 256
RUN = 4
VECTOR_SHARE = 256
NEG_MAX, ROW_SUM, INVERSE, STATS = 0, 8, 16, 24


def tile_picked_zpq_soft_p_kernel(
    tc, x_words, x_scales, e_words, e_scales, f_words, f_scales, hT, gT, rT, offs, code2, code3, out
):
    nc = tc.nc
    words_in = (x_words, e_words, f_words)
    scales_in = (x_scales, e_scales, f_scales)
    queries = (hT, gT, rT)
    lists_in = (offs, code2, code3)

    with ExitStack() as ctx:
        keep = ctx.enter_context(tc.tile_pool(name="keep", bufs=1))
        shared = ctx.enter_context(tc.tile_pool(name="shared", bufs=1))
        psum = ctx.enter_context(tc.psum_pool(name="psum", bufs=1))

        after_bytes = "last scale table, then last word table"
        after_words = "first word table, then last queries"

        lists = [keep.tile([P, S // 16], U16, name="list%d" % a) for a in range(PARTS)]
        byte_tags = ["byte_window0", "byte_window1", after_bytes]
        byte_window = [
            keep.tile([P, T], U8, name="byte_window%d" % a, tag=byte_tags[a], align_bytes=WIDE) for a in range(PARTS)
        ]
        picked_bytes = keep.tile([P, PARTS * S], U8, name="picked_bytes", align_bytes=WIDE)
        moving_scales = keep.tile([P, PARTS * S], U8, name="moving_scales", align_bytes=WIDE)

        for a in range(PARTS):
            nc.scalar.dma_start(out=byte_window[a][SCALES_AT:P, :].bitcast(I32), in_=scales_in[a][0].bitcast(I32))
        for a in range(PARTS):
            nc.vector.memset(byte_window[a][0:SCALES_AT, :].bitcast(I32), 0)
        nc.vector.memset(moving_scales[:].bitcast(I32), 0)

        word_window = {}
        raw = {}

        def load_words(a, tag):
            word_window[a] = keep.tile([P, T], I32, name="word_window%d" % a, tag=tag, align_bytes=WIDE)
            nc.sync.dma_start(out=word_window[a][:], in_=words_in[a][0].rearrange("p n t -> p (n t)").bitcast(I32))

        def load_queries(part, first_tile, tiles, room):
            rows = room.rearrange("p (t c) -> p t c", t=PACK)
            columns = queries[part][:, first_tile * M : (first_tile + tiles) * M]
            nc.sync.dma_start(out=rows, in_=columns.rearrange("(p t) c -> p t c", t=PACK))
            for u in range(tiles):
                raw[(part, first_tile + u)] = rows[:, :, u * M : (u + 1) * M]

        picked_words = {}

        def gather_words(a):
            picked_words[a] = keep.tile([P, S], U32, name="picked_words%d" % a, align_bytes=WIDE)
            nc.vector.tensor_copy(picked_words[a][:], word_window[a][:].bitcast(U32).indirect(lists[a][:]))

        for a in range(PARTS):
            nc.sync.dma_start(lists[a][:], lists_in[a])
        word_tags = [after_words, "word_window1"]
        for a in range(LAST):
            load_words(a, word_tags[a])
            whole = keep.tile([P, PACK * J], F32, name="queries%d" % a, align_bytes=WIDE)
            load_queries(a, 0, TILES, whole[:])

        for a in range(PARTS):
            nc.vector.tensor_copy(picked_bytes[:, a * S : (a + 1) * S], byte_window[a][:].indirect(lists[a][:]))
        for r in range(PACK):
            nc.sync.dma_start(
                out=moving_scales[r:P:QUAD, :].bitcast(I32), in_=picked_bytes[SCALES_AT + r : P : PACK, :].bitcast(I32)
            )

        load_words(LAST, after_bytes)
        gather_words(0)
        last_queries = keep.tile([P, PACK * J], F32, name="last_queries", tag=after_words, align_bytes=WIDE)
        for b in range(TILES):
            load_queries(LAST, b, 1, last_queries[:, b * PACK * M : (b + 1) * PACK * M])

        scores = [psum.tile([M, S], F32, name="scores%d" % b) for b in range(TILES)]

        def multiply(part, b):
            grouped = keep.tile([P, M * PACK], BF16, name="grouped%d%d" % (part, b), align_bytes=64)
            src = raw[(part, b)].rearrange("p t (c i) -> p c t i", i=RUN)
            dst = grouped[:].rearrange("p (c i t) -> p c t i", i=RUN, t=PACK)
            if (part, b) == (LAST - 1, TILES - 1):
                nc.vector.tensor_copy(out=dst, in_=src)
            elif (part, b) == (LAST, TILES - 1):
                src = raw[(part, b)].rearrange("p t c -> p c t")
                dst = grouped[:].rearrange("p (c t) -> p c t", t=PACK)
                nc.gpsimd.tensor_scalar(out=dst, in0=src, scalar1=1.0, scalar2=0.0, op0=ALU.mult, op1=ALU.add)
            else:
                nc.scalar.activation(out=dst, in_=src, func=ACT.Copy)
            codes = keep.tile([P, M], U32, name="codes%d%d" % (part, b), align_bytes=64)
            if (part, b) == (LAST, TILES - 1):
                scales = shared.tile([P, M], U8, name="last_scales", offset=64, align_bytes=64)
            else:
                scales = keep.tile([P, M], U8, name="scales%d%d" % (part, b), align_bytes=64)
            nc.vector.quantize_mx(out=codes[:].bitcast(FP8X4), scales=scales[:], in_=grouped[:])
            nc.tensor.matmul_mx(
                out=scores[b][:],
                lhsT=codes[:].bitcast(FP8X4),
                lhsT_scale=scales[:],
                rhs=picked_words[part][:].bitcast(FP8X4),
                rhs_scale=moving_scales[:, part * S : (part + 1) * S],
                start=part == 0,
                stop=part == LAST,
            )

        powers = {}
        stats = {}

        def exponents(b):
            if b == 0:
                neg_max = shared.tile([P, 32], F32, name="neg_max0", offset=0)[:, 0:1]
            elif b == 2:
                neg_max = shared.tile([P, 1], F32, name="neg_max2", offset=0)[:]
            else:
                neg_max = keep.tile([P, 1], F32, name="neg_max%d" % b, tag="odd maxima")[:]
            stats[b] = keep.tile([P, STATS], F32, name="stats%d" % b)
            powers[b] = keep.tile([P, S], F32, name="powers%d" % b, align_bytes=WIDE)
            nc.vector.tensor_reduce(out=neg_max, in_=scores[b][:], axis=mybir.AxisListType.X, op=ALU.max, negate=True)
            row_sum = stats[b][:, ROW_SUM : ROW_SUM + 1]
            nc.scalar.activation(out=powers[b][:], in_=scores[b][:], func=ACT.Exp, bias=neg_max, accum_out=row_sum)

        def normalise(b):
            inverse = stats[b][:, INVERSE : INVERSE + 1]
            nc.vector.reciprocal(out=inverse, in_=stats[b][:, ROW_SUM : ROW_SUM + 1])
            rows = slice(b * M, (b + 1) * M)
            result = keep.tile([P, S], F32, name="result%d" % b, align_bytes=WIDE)
            if b < 2:
                nc.gpsimd.tensor_scalar(
                    out=result[:], in0=powers[b][:], scalar1=inverse, scalar2=0.0, op0=ALU.mult, op1=ALU.add
                )
                nc.sync.dma_start(out=out[rows, :], in_=result[:])
            elif b < TILES - 1:
                nc.vector.tensor_scalar(out=result[:], in0=powers[b][:], scalar1=inverse, scalar2=None, op0=ALU.mult)
                nc.sync.dma_start(out=out[rows, :], in_=result[:])
            else:
                left, right = slice(0, VECTOR_SHARE), slice(VECTOR_SHARE, S)
                rest = keep.tile([P, S], F32, name="result_rest", align_bytes=WIDE)
                nc.vector.tensor_scalar(
                    out=result[:, left], in0=powers[b][:, left], scalar1=inverse, scalar2=None, op0=ALU.mult
                )
                nc.scalar.activation(out=rest[:, right], in_=powers[b][:, right], func=ACT.Copy, scale=inverse)
                nc.sync.dma_start(out=out[rows, left], in_=result[:, left])
                nc.scalar.dma_start(out=out[rows, right], in_=rest[:, right])

        for part in range(LAST):
            if part > 0:
                gather_words(part)
            for b in range(TILES):
                multiply(part, b)
        gather_words(LAST)
        for b in range(TILES - 1):
            multiply(LAST, b)
        exponents(0)
        normalise(0)
        multiply(LAST, TILES - 1)
        for b in range(1, TILES):
            exponents(b)
            normalise(b)
